import numpy as np, ml_dtypes
CORES = [66,74,82,90,194,202,210,218]
N = 8
BF = ml_dtypes.bfloat16
def f(rng, *shape):
    return (rng.standard_normal(shape, dtype=np.float32) * np.exp2(rng.integers(-2, 3, shape[:-1] + (1,)))).astype(BF)
def wide(rng, *shape):
    v = f(rng, *shape).astype(np.float32); k = shape[:-2] + (1, shape[-1])
    return (v * np.exp2(rng.integers(-6, 7, k)) * (rng.random(k) > 0.0625)).astype(BF)
def gentries(a):
    return np.ascontiguousarray(a.reshape(8, 16, -1).transpose(0, 2, 1)).reshape(8, -1)
def gtable(e):
    e = np.asarray(e); return np.ascontiguousarray(e.reshape(8, -1, 16).transpose(0, 2, 1)).reshape(128, -1).astype(np.int32)
P, E, S, W, TT, CAPP = 3, 256, 2048, 128, 2048, 48
I, LS = N * S, 11
def events(x):
    return np.stack([gentries(u) for u in x]).reshape(N, 8, P, E).transpose(0, 2, 1, 3).astype(np.int64)
def unevents(e):
    return np.stack([gtable(u) for u in e.transpose(0, 2, 1, 3).reshape(N, 8, P * E)])
def shifts(sh, t):
    return np.take_along_axis(sh.astype(np.int64).reshape(N, 8, P, TT).transpose(0, 2, 1, 3), t, -1)
def evenly(rng):
    c = rng.multinomial(E, np.full(N, 2.0 ** -3), (P, 8, N)); x = np.sum(np.maximum(c - CAPP, 0), -1); c = np.minimum(c, CAPP)
    while x.any():
        i = np.argmin(c, -1)[..., None]; np.put_along_axis(c, i, np.take_along_axis(c, i, -1) + (x > 0)[..., None], -1); x = x - (x > 0)
    return c
def fully(rng):
    a = np.array(([CAPP] * (E // CAPP) + [E % CAPP] + [0] * N)[:N]); o = np.argsort(rng.random((P, 8, N, N)), -1)
    o[1::2] = o[1::2, :, :1].copy()
    return a[o]
def draw(rng, cnt, t, sh, v, crowd=False):
    pl = np.zeros((N, P, 8, E), np.int64)
    for k in range(P):
        for g in range(8):
            got = [[] for r in range(N)]
            for q in range(N):
                m = int(np.sum(cnt[k, g, :, q])); h = m // 2
                s = rng.permutation(np.append(np.arange(m - h), np.arange(S - h, S))) if crowd else rng.permutation(S)[:m]
                for r, u in enumerate(np.split(s, np.add.accumulate(cnt[k, g, :, q])[:-1])): got[r].append(u + S * q)
            for r in range(N): pl[r, k, g] = rng.permutation(np.concatenate(got[r]))
    v = v.astype(np.float32) * (1 + rng.random((N, 128, S), dtype=np.float32))
    rate = ((1 + rng.random((N, 128, 1))) * np.exp2(-rng.integers(7, 14, (N, 128, 1)))).astype(np.float32)
    return {"v": v, "last": rng.integers(-4096, 1, (N, 8, S)).astype(np.int32), "rate": rate, "sh": sh.astype(np.int32),
            "pix": unevents((pl - shifts(sh, t)) & (I - 1)), "tm": unevents(t), "pol": unevents(2 * rng.integers(0, 2, (N, P, 8, E)) - 1)}
def setup_inputs(rng):
    return draw(rng, evenly(rng), rng.integers(0, TT, (N, P, 8, E)), rng.integers(0, I, (N, 8, P * TT)), f(rng, N, 128, S))
def setup_inputs_full(rng):
    return draw(rng, fully(rng), rng.integers(0, TT, (N, P, 8, E)), rng.integers(0, I, (N, 8, P * TT)), f(rng, N, 128, S))
def setup_inputs_ends(rng):
    t = np.array([0, 1, TT - 1])[rng.integers(0, 3, (N, P, 8, E))]
    d = draw(rng, evenly(rng), t, rng.integers(0, I, (N, 8, P * TT)), f(rng, N, 128, S), True)
    d["last"] = (-4096 * rng.integers(0, 2, (N, 8, S))).astype(np.int32); return d
def setup_inputs_still(rng):
    t = np.repeat(rng.integers(0, TT, (N, P, 8, 1)), E, -1); sh = rng.integers(0, I, (N, 8, P * TT)); sh[rng.permutation(N)[:2]] = 0
    return draw(rng, evenly(rng), t, sh, f(rng, N, 128, S))
def setup_inputs_spread(rng):
    return draw(rng, evenly(rng), rng.integers(0, TT, (N, P, 8, E)), rng.integers(0, I, (N, 8, P * TT)), wide(rng, N, 128, S))
def check_inputs(d):
    bad = [] if np.isfinite(d["v"]).all() else ["v finite"]
    for a, lo, hi in (("rate", 2.0 ** -14, 2.0 ** -6), ("last", -4096, 0), ("sh", 0, I - 1), ("pix", 0, I - 1), ("tm", 0, TT - 1)):
        if not ((d[a] >= lo) & (d[a] <= hi)).all(): bad.append(a + " range")
    if not ((d["pol"] == 1) | (d["pol"] == -1)).all(): bad.append("pol is 1 or -1")
    if bad: return bad
    pl = (events(d["pix"]) + shifts(d["sh"], events(d["tm"]))) & (I - 1)
    r, k, g = np.arange(N)[:, None, None, None], np.arange(P)[None, :, None, None], np.arange(8)[None, None, :, None]
    if np.bincount(((((r * P + k) * 8 + g) * N) + (pl >> LS)).reshape(-1)).max() > CAPP: bad.append("CAPP")
    if np.unique((k * 8 + g) * I + pl).size != pl.size: bad.append("places of a packet differ")
    return bad
def reference(v, last, rate, sh, pix, tm, pol):
    V = v.astype(np.float64).reshape(N, 8, 16, S); L = last.astype(np.int64); a = rate.astype(np.float64).reshape(N, 8, 16)
    t, w = events(tm), events(pol); pl = (events(pix) + shifts(sh, t)) & (I - 1)
    y = np.zeros((N, 8, 16, P, E), np.float64); g = np.arange(8)[None, :, None]
    for k in range(P):
        q, c, now = pl[:, k] >> LS, pl[:, k] & (S - 1), TT * k + t[:, k]
        V[q, g, :, c] = V[q, g, :, c] * np.exp(-a[q, g] * (now - L[q, g, c])[..., None]) + w[:, k][..., None]
        L[q, g, c] = now
        s = np.zeros((N, 8, E, 16))
        for e in (-1, 1, -W, W): s = s + V[q, g, :, np.minimum(np.maximum(c + e, 0), S - 1)]
        y[:, :, :, k] = s.transpose(0, 1, 3, 2)
    return {"y": y.reshape(N, 128, P * E).astype(np.float32)}

from concourse.bass import DstId, RemoteDMATransfer
from concourse.mybir import AluOpType as Op, ActivationFunctionType as Fn

N, P, E, S, W, TT, CAP = 8, 3, 256, 2048, 128, 2048, 48
NS = N * CAP
F, B, I, U = "float32", "bfloat16", "int32", "uint16"

ROUTE = {"e0": "self", "e1": "pair", "e2": "pair", "a0": "pair", "a1": "tail"}

_SB = {
    I: {"tml": [3, 16], "shw": [384], "raw": [8, 48], "lw": [S + NS], "pi": [1], "ic": [9], "lh": [6, 16], "vi": [72], "ci": [72]},
    F: {"rat": [1], "vw": [S + NS], "fc": [9], "cc": [16], "jj": [160], "j8": [136], "j16": [128], "jt": [24], "tab16": [16],
        "tabd": [24], "b3": [136], "idn": [128], "zs": [6, 16], "mk": [768], "yy": [768], "u1": [384], "u2": [384],
        "em": [72], "du": [72], "ow": [72], "aa": [3 * NS], "ww": [3 * NS], "dt": [3 * NS], "ee": [3 * NS], "tv": [3 * NS],
        "gg": [11 * NS], "ans": [3 * NS], "ra": [3 * NS], "yo": [768]},
    B: {"zer": [128], "rx": [128], "fx": [256], "fr": [256], "bs": [136], "b2": [144], "ga": [128], "gw": [128],
        "zz": [6, 32], "zt": [6, 32], "rb": [8, 48], "rr": [8, 48], "xb": [384], "xr": [384], "sm": [384], "st": [384],
        "pp": [384], "dd": [768], "snd": [3 * NS], "ev": [3 * NS]},
    U: {"of": [96], "sl": [48], "sn": [48], "cu": [72], "ou": [72], "nu": [288]},
}
SCRATCH = {n: ("sbuf", [128] + s, d) for d, bufs in _SB.items() for n, s in bufs.items()}
PSUM = ("px0", "px1", "pd0", "pd1", "ps", "pn", "pa", "pw")
SCRATCH.update({n: ("psum", [128, 32, 16] if n[1] == "d" else [128, 512], F) for n in PSUM})
MSGS = ["e0", "e1", "e2", "a0", "a1"]
SEMAPHORES = (["cv", "ca", "ct", "cg", "d_tm", "d_sh0", "d_sh1", "d_sh2", "d_raw", "d_rate", "d_v", "d_l", "d_y", "sent", "sent0"]
              + ["ar_" + m for m in MSGS] + ["h_" + m for m in MSGS])


def helpers(rc, T, topo):
    hs = [c for c in topo.cores_of(rc) if T.rank_of(c) is None and all(topo.may_write(c, d) for d in T.cores if d != rc)]
    return sorted(hs, key=lambda c: (topo.die(c) == topo.die(rc), c))


def parts(m, r):
    if ROUTE[m] == "self":
        return [], [q for q in range(N) if q != r]
    if ROUTE[m] == "pair":
        return [list(range(0, N // 2)), list(range(N // 2, N))], []
    far = N // 2 if r < N // 2 else 0
    near = N // 2 - far
    return ([list(range(far, far + N // 4)), list(range(far + N // 4, far + N // 2))],
            [q for q in range(near, near + N // 2) if q != r])


def share(src, dst, n, topo):
    k = 1
    while 2 * k * n <= len(topo.engines(src, dst)):
        k *= 2
    return k


def arrivals(m, q, T, topo):
    n = 0
    for r in range(N):
        if r != q:
            hp, sp = parts(m, r)
            for qs in hp + [sp]:
                if q in qs:
                    n += share(T.cores[r], T.cores[q], len([x for x in qs if x != r]), topo)
    return n


def sides(T, m):
    k = int(m[1])
    src, dst, w = (T.snd, T.ev, CAP) if m[0] == "e" else (T.ans, T.ra, CAP * (k + 1))
    return (lambda a, b: src[:, NS * k + w * a:NS * k + w * b]), (lambda r: dst[:, NS * k + w * r:NS * k + w * r + w])


def spread(g, core, r, m, qs, T, topo, sem):
    src, dst = sides(T, m)
    qs = sorted([q for q in qs if q != r], key=lambda q: (q - r) % N)
    trs, n = [], 0
    for q in qs:
        k = share(core, T.cores[q], len(qs), topo)
        rid, pid = topo.addr(T.cores[q], core)
        es = topo.engines(core, T.cores[q])[n:n + k]
        n += k
        trs.append(RemoteDMATransfer(dst_ids=[DstId(rid=rid, pnc=pid)], dma_engine_mask=sum(1 << e for e in es),
                                     remote_sem=T.sem["ar_" + m], src=src(q, q + 1), dst=dst(r)))
    g.remote_dma_fused(trs, local_sem=sem)
    return n


def hand_engines(core, h, j, m, T, topo):
    far = [d for d in T.cores if d != core][0]
    es = topo.engines(core, h)
    if m[0] == "e":
        es = [e for e in es if e not in topo.engines(core, far)]
    return es[j * len(es) // 2:(j + 1) * len(es) // 2]


def helper_program(g, core, T, topo):
    for r, rc in enumerate(T.cores):
        if core not in topo.cores_of(rc):
            continue
        hs = helpers(rc, T, topo)
        sent = 0
        for m in MSGS:
            for j, qs in enumerate(parts(m, r)[0]):
                if hs[j] == core:
                    g.wait_ge(T.sem["h_" + m], len(hand_engines(rc, core, j, m, T, topo)))
                    sent += spread(g, core, r, m, qs, T, topo, T.sem.sent)
        if sent:
            g.wait_ge(T.sem.sent, sent)


def rank_program(g, core, T, topo):
    r = T.rank_of(core)
    if r is None:
        helper_program(g, core, T, topo)
        return
    Q = {"v": g.vector, "a": g.scalar, "t": g.tensor, "g": g, "s": g.sync}
    own = {"v": "cv", "a": "ca", "t": "ct", "g": "cg"}
    cnt = {"cv": 0, "ca": 0, "ct": 0, "cg": 0}
    seen = {q: {} for q in Q}
    lastw, readers, touched = {}, {}, {}

    def wait(q, ev):
        if seen[q].get(ev[0], 0) < ev[1]:
            Q[q].wait_ge(T.sem[ev[0]], ev[1])
            seen[q][ev[0]] = ev[1]

    def before(q, reads, writes):
        need = {}
        def add(ev):
            need[ev[0]] = max(need.get(ev[0], 0), ev[1])
        for t in list(reads) + list(writes):
            if t in PSUM:
                for q2, ev in touched.get(t, {}).items():
                    if q2 != q:
                        add(ev)
            elif t in lastw:
                add(lastw[t])
        for t in writes:
            for ev in readers.get(t, []):
                add(ev)
        for s, c in need.items():
            wait(q, (s, c))

    def after(q, ev, reads, writes):
        for t in list(reads) + list(writes):
            if t in PSUM:
                touched.setdefault(t, {})[q] = ev
        for t in reads:
            if t not in PSUM:
                readers.setdefault(t, []).append(ev)
        for t in writes:
            if t not in PSUM:
                lastw[t] = ev
                readers[t] = []

    def op(q, reads, writes, fn):
        before(q, reads, writes)
        s = own[q]
        fn().then_inc(T.sem[s], 1)
        cnt[s] += 1
        after(q, (s, cnt[s]), reads, writes)

    dcnt = {}

    def dma(q, sem, total, reads, writes, out, in_):
        before(q, reads, writes)
        Q[q].dma_start(out, in_).then_inc(T.sem[sem], 16)
        dcnt[sem] = 16 * total
        after(q, (sem, 16 * total), reads, writes)

    V, A, PE = g.vector, g.scalar, g.tensor
    def ts(out, in0, s1, op0, s2=None, op1=None):
        if op1 is None:
            return V.tensor_scalar(out, in0, s1, None, op0)
        return V.tensor_scalar(out, in0, s1, s2, op0, op1)

    op("v", [], ["raw0"], lambda: V.memset(T.raw[:], 0))
    dma("s", "d_tm", 1, [], ["tml"], T.tml[:], T.tm[:])
    dma("s", "d_sh0", 1, [], ["shw0"], T.shw[:, 0:128], T.sh[:, 0:TT])
    for q, t, src in (("a", 6, T.pix), ("a", 7, T.pix), ("a", 2, T.tm), ("s", 3, T.tm), ("s", 4, T.pol)):
        dma(q, "d_raw", 5, ["raw0"], ["raw_%d" % t], T.raw[t::8], src[:])
    for k in range(1, P):
        dma("s", "d_sh%d" % k, 1, [], ["shw%d" % k], T.shw[:, 128 * k:128 * k + 128], T.sh[:, TT * k:TT * k + TT])
    RAW = ["raw_%d" % t for t in (6, 7, 2, 3, 4)]
    for o in range(16):
        dma("a" if o % 4 == 3 else "s", "d_l", 16, [], ["lw_%d" % o], T.lw[o::16, 0:S], T.last[:])
    lastw["lw"] = ("d_l", 256)
    dma("s", "d_rate", 1, [], ["rat"], T.rat[:], T.rate[:])
    dma("s", "d_v", 2, [], ["vw_a"], T.vw[:, 0:S // 2], T.v[:, 0:S // 2])

    fl = dict(allow_small_or_imprecise_dtypes=True)
    op("g", [], ["pi"], lambda: g.iota(T.pi[:], [[0, 1]], 0, 1))
    op("g", [], ["jj"], lambda: g.iota(T.jj[:], [[1, 160]], -16, 0, **fl))
    op("g", [], ["j8"], lambda: g.iota(T.j8[:], [[8, 17], [0, 8]], -8, 0, **fl))
    op("g", [], ["zer"], lambda: g.iota(T.zer[:], [[0, 128]], 0, 0, **fl))
    for k in range(P):
        op("g", [], ["snd%d" % k], lambda k=k: g.iota(T.snd[:, NS * k:NS * k + NS], [[0, NS]], 0, 0, **fl))
    op("g", [], ["j16"], lambda: g.iota(T.j16[:], [[16, 8], [0, 16]], 0, 0, **fl))
    op("g", [], ["jt"], lambda: g.iota(T.jt[:], [[16, 24]], S, 0, **fl))
    masks = [8, 14, 16, 15, 7, 1, 120, 112, 127]
    for j, m in enumerate(masks):
        op("v", ["pi"], ["ic%d" % j], lambda j=j, m=m: ts(T.ic[:, j:j + 1], T.pi[:], m, Op.bitwise_and))
    op("v", ["ic%d" % j for j in range(9)], ["fc"], lambda: V.tensor_copy(T.fc[:], T.ic[:]))
    fc = lambda j: T.fc[:, j:j + 1]
    H8, O14, G16, O, R8, B1, P8, P16, PF = [fc(j) for j in range(9)]
    cc = lambda j: T.cc[:, j:j + 1]
    HB, CB, MH = (cc(0), cc(3)), (cc(1), cc(4)), (cc(2), cc(5))
    R6, SIGN, NEGM, INI0, INI, GWC, GAC, WV = [cc(j) for j in range(6, 14)]
    op("v", ["fc"], ["c0"], lambda: ts(T.cc[:, 0:3], T.fc[:, 0:3], 0.0, Op.is_equal))
    op("v", ["fc"], ["c5"], lambda: ts(cc(5), G16, 16.0, Op.is_equal))
    op("v", ["fc", "jj"], ["tab16"], lambda: ts(T.tab16[:], T.jj[:, 16:32], O, Op.is_equal))
    op("v", ["fc"], ["c3"], lambda: ts(T.cc[:, 3:5], T.fc[:, 0:2], 8.0, Op.is_equal))
    op("v", ["fc"], ["r6"], lambda: ts(R6, R8, 6.0, Op.is_ge))
    op("v", ["fc"], ["sign"], lambda: ts(SIGN, H8, -0.25, Op.mult, 1.0, Op.add))
    op("v", ["fc"], ["negm"], lambda: ts(NEGM, R8, -2048.0, Op.mult, -9215.5, Op.add))
    op("v", ["fc"], ["ini0"], lambda: ts(INI0, H8, 6.125, Op.mult, -193.0, Op.add))
    op("v", ["fc", "j8"], ["b3"], lambda: ts(T.b3[:], T.j8[:], P16, Op.is_equal))
    op("v", ["fc", "ini0"], ["ini"], lambda: ts(INI, R8, 48.0, Op.mult, INI0, Op.add))
    op("v", ["fc", "j8", "r6"], ["rx"], lambda: ts(T.rx[:], T.j8[:, 8:136], P8, Op.is_equal, R6, Op.mult))
    for b in range(2):
        op("v", ["fc", "jj", "c0", "c3"], ["fr_%d" % b], lambda b=b: ts(
            T.fr[:, 128 * b:128 * b + 128], T.jj[:, 16 + 8 * b:144 + 8 * b], PF, Op.is_equal, HB[b], Op.mult))

    op("v", ["tml"], ["lh0"], lambda: ts(T.lh[:, 0:3, :], T.tml[:], 127, Op.bitwise_and))
    op("v", ["tml"], ["lh1"], lambda: ts(T.lh[:, 3:6, :], T.tml[:], 7, Op.logical_shift_right))
    for h in range(2):
        op("v", ["lh0", "lh1", "c0", "c5"], ["zz%d" % h], lambda h=h: ts(T.zz[:, :, 16 * h:16 * h + 16], T.lh[:], MH[h], Op.mult))
    op("v", ["zz0", "zz1"], ["zt"], lambda: V.transpose(T.zt[:], T.zz[:]))
    op("v", ["zt"], ["zs"], lambda: V.tensor_tensor(T.zs[:], T.zt[:, :, 0:16], T.zt[:, :, 16:32], Op.add))
    op("v", ["zs"], ["of"], lambda: V.tensor_copy(T.of[:], T.zs[:]))

    def cuts(k):
        return ((0, 1), (1, 2)) if k == 0 else ((0, 2),)

    def picks(k):
        for a, b in cuts(k):
            op("a", ["of", "tab16"], ["mk%d%d" % (k, h) for h in range(a, b)], lambda: A.activation(
                T.mk[:, E * k + 128 * a:E * k + 128 * b],
                T.tab16[:, 0:16].indirect(T.of[:, 48 + 16 * k + 8 * a:48 + 16 * k + 8 * b]), Fn.Identity))

    def ygather(k):
        for a, b in cuts(k):
            c = slice(E * k + 128 * a, E * k + 128 * b)
            op("v", ["of", "shw%d" % k] + ["mk%d%d" % (k, h) for h in range(a, b)], ["yy%d%d" % (k, h) for h in range(a, b)],
               lambda: V.tensor_tensor(T.yy[:, c], T.shw[:, 128 * k:128 * k + 128].indirect(T.of[:, 16 * k + 8 * a:16 * k + 8 * b]),
                                       T.mk[:, c], Op.mult))

    def digits(k):
        c = slice(16 * k, 16 * k + 16)
        op("v", RAW + ["fc"], ["rb%d" % k], lambda: ts(T.rb[:, :, c], T.raw[:, :, c], B1, Op.mult))
        op("v", RAW + ["rb%d" % k], ["rr%d" % k], lambda: V.tensor_tensor(T.rr[:, :, c], T.raw[:, :, c], T.rb[:, :, c], Op.subtract))

    def xsum(k):
        px = "px%d" % (k % 2)
        op("t", ["b3", "yy%d0" % k], [px], lambda: PE.matmul(T[px][:, 0:128], T.b3[:, 8:136], T.yy[:, E * k:E * k + 128], True, False))
        op("t", ["b3", "yy%d1" % k], [px], lambda: PE.matmul(T[px][:, 0:128], T.b3[:, 0:128], T.yy[:, E * k + 128:E * k + 256], False, False))
        op("t", ["rx", "rr%d" % k], [px], lambda: PE.matmul(T[px][:, 0:128], T.rx[:], T.rr[:, :, 16 * k:16 * k + 16], False, True))

    def ranges(k):
        px, c = "px%d" % (k % 2), slice(128 * k, 128 * k + 128)
        op("a", [px, "negm"], ["u1%d" % k], lambda: A.activation(T.u1[:, c], T[px][:, 0:128], Fn.Abs, bias=NEGM))
        op("a", [px, "fc"], ["xb%d" % k], lambda: A.activation(T.xb[:, c], T[px][:, 0:128], Fn.Identity, scale=B1))
        op("a", ["u1%d" % k], ["u2%d" % k], lambda: A.activation(T.u2[:, c], T.u1[:, c], Fn.Abs, bias=-8192.0))

    def ranking(k):
        px, pd, c = "px%d" % (k % 2), "pd%d" % (k % 2), slice(128 * k, 128 * k + 128)
        op("v", [px, "xb%d" % k], ["xr%d" % k], lambda: V.tensor_tensor(T.xr[:, c], T[px][:, 0:128], T.xb[:, c], Op.subtract))
        def rund():
            for h in range(2):
                PE.matmul(T[pd][:, 0:16, 8 * h:8 * h + 8], T.fr[:, 128 * h:128 * h + 128], T.rr[:, :, 16 * k:16 * k + 16], True, False)
                last = PE.matmul(T[pd][:, 0:16, 8 * h:8 * h + 8], T.fx[:, 128 * h:128 * h + 128], T.xr[:, c], False, True)
            return last
        op("t", ["fr", "fx", "rr%d" % k, "xr%d" % k], [pd], rund)
        op("a", [pd], ["dd%d" % k], lambda: A.activation(T.dd[:, E * k:E * k + E], T[pd][:, 0:16, :], Fn.Identity))
        op("v", ["u2%d" % k, "sign"], ["sm%d" % k], lambda: ts(T.sm[:, c], T.u2[:, c], 1024.0, Op.is_lt, SIGN, Op.mult))
        op("v", ["sm%d" % k, "zer", "ini"], ["st%d" % k], lambda: V.tensor_tensor_scan(T.st[:, c], T.sm[:, c], T.zer[:], INI, Op.add, Op.add))
        op("v", ["sm%d" % k, "st%d" % k], ["pp%d" % k], lambda: V.tensor_tensor(T.pp[:, c], T.st[:, c], T.sm[:, c], Op.mult))
        def runs():
            for u in range(8):
                last = PE.matmul(T.ps[:, 0:16], T.bs[:, 8 - u:136 - u], T.pp[:, 128 * k + u:128 * k + 128:8], u == 0, u == 7)
            return last
        op("t", ["bs", "pp%d" % k], ["ps"], runs)

    def natural(k):
        def runn():
            for u in range(8):
                last = PE.matmul(T.pn[:, 16 * k:16 * k + 16], T.bs[:, 8 - u:136 - u],
                                 T.pp[:, 128 * k + 16 * u:128 * k + 16 * u + 16], u == 0, u == 7)
            return last
        op("t", ["bs", "pp%d" % k], ["pn"], runn)

    sent = {"sent": 0, "sent0": 0}
    hs = helpers(core, T, topo)

    def hand(m, reads):
        src = sides(T, m)[0]
        trs = []
        for j, qs in enumerate(parts(m, r)[0]):
            es = hand_engines(core, hs[j], j, m, T, topo)
            rid, pid = topo.addr(hs[j], core)
            ap = src(qs[0], qs[-1] + 1)
            trs.append(RemoteDMATransfer(dst_ids=[DstId(rid=rid, pnc=pid)], dma_engine_mask=sum(1 << e for e in es),
                                         remote_sem=T.sem["h_" + m], src=ap, dst=ap))
            sent["sent"] += len(es)
        if trs:
            before("g", reads, [])
            g.remote_dma_fused(trs, local_sem=T.sem.sent)

    def direct(m, reads):
        qs = parts(m, r)[1]
        if qs:
            before("g", reads, [])
            s = "sent0" if m == "e0" else "sent"
            sent[s] += spread(g, core, r, m, qs, T, topo, T.sem[s])

    def place(k):
        op("v", ["ps"], ["sl%d" % k], lambda: ts(T.sl[:, 16 * k:16 * k + 16], T.ps[:, 0:16], 192.0, Op.add))
        op("v", ["sl%d" % k, "dd%d" % k], ["snd%d" % k], lambda: V.tensor_copy(
            T.snd[:, NS * k:NS * k + NS].indirect(T.sl[:, 16 * k:16 * k + 16]), T.dd[:, E * k:E * k + E]))
        hand("e%d" % k, ["snd%d" % k])
        direct("e%d" % k, ["snd%d" % k])
        lastw["ev%d" % k] = ("ar_e%d" % k, arrivals("e%d" % k, r, T, topo))

    def mine(k):
        c = slice(NS * k + CAP * r, NS * k + CAP * r + CAP)
        op("a", ["snd%d" % k], ["evo%d" % k], lambda: A.activation(T.ev[:, c], T.snd[:, c], Fn.Identity))

    picks(0); picks(1)
    for b in range(2):
        op("v", ["fc", "jj", "c0", "c3"], ["fx_%d" % b], lambda b=b: ts(
            T.fx[:, 128 * b:128 * b + 128], T.jj[:, 16 + 8 * b:144 + 8 * b], PF, Op.is_equal, CB[b], Op.mult))
    op("v", ["fc", "jj", "sign"], ["bs"], lambda: ts(T.bs[:], T.jj[:, 8:144], P8, Op.is_equal, SIGN, Op.mult))
    lastw["fx"] = lastw["fr"] = lastw["bs"]
    ygather(0); digits(0); xsum(0); ranges(0); digits(1)
    ranking(0); picks(2); ygather(1); xsum(1); ranges(1); place(0)
    wait("s", ("sent0", sent["sent0"]))
    dma("s", "d_v", 2, [], ["vw"], T.vw[:, S // 2:S], T.v[:, S // 2:S])
    ranking(1); ygather(2); digits(2); xsum(2); ranges(2); place(1); ranking(2)
    op("v", ["fc"], ["gwc"], lambda: ts(GWC, O, 4.0, Op.is_equal))
    op("v", ["fc"], ["gac"], lambda: ts(GAC, O14, 2.0, Op.is_equal))
    op("v", ["gwc", "c0"], ["wv"], lambda: ts(WV, GWC, 65536.0, Op.mult, CB[0], Op.add))
    op("v", ["fc", "jt"], ["tabd"], lambda: ts(T.tabd[:], T.jt[:], O, Op.add))
    place(2)
    op("v", ["fc", "jj", "wv"], ["b2"], lambda: ts(T.b2[:], T.jj[:, 0:144], P16, Op.is_equal, WV, Op.mult))
    op("v", ["fc", "j16", "gac"], ["ga"], lambda: ts(T.ga[:], T.j16[:], P16, Op.is_equal, GAC, Op.mult))
    op("v", ["fc", "j16", "gwc"], ["gw"], lambda: ts(T.gw[:], T.j16[:], P16, Op.is_equal, GWC, Op.mult))
    op("v", ["fc", "jj"], ["idn"], lambda: ts(T.idn[:], T.jj[:, 16:144], PF, Op.is_equal))
    for k in range(P):
        natural(k)
        mine(k)
    op("v", ["pn"], ["sn0"], lambda: ts(T.sn[:, 0:16], T.pn[:, 0:16], 192.0, Op.add))
    for k in (1, 2):
        op("v", ["pn"], ["sn%d" % k], lambda k=k: ts(T.sn[:, 16 * k:16 * k + 16], T.pn[:, 16 * k:16 * k + 16],
                                                     2.0, Op.mult, 383.0 + k, Op.add))

    def places(k):
        def runl():
            for u in range(16):
                last = PE.matmul(T.ps[:, 0:24], T.b2[:, 16 - u:144 - u], T.ev[:, NS * k + u:NS * k + NS:16], u == 0, u == 15)
            return last
        op("t", ["ev%d" % k, "evo%d" % k, "b2"], ["ps"], runl)

    def times(k):
        e0 = NS * k
        rd = ["ev%d" % k, "evo%d" % k]
        pa, pw = ("pa", "pw") if k < 2 else ("pd0", "pd1")
        oa, ow = (T.pa[:, 0:NS], T.pw[:, 0:NS]) if k < 2 else (T.pd0[:, 0:24, :], T.pd1[:, 0:24, :])
        op("t", rd + ["ga"], [pa], lambda: PE.matmul(oa, T.ga[:], T.ev[:, e0:e0 + NS], True, True))
        op("t", rd + ["gw"], [pw], lambda: PE.matmul(ow, T.gw[:], T.ev[:, e0:e0 + NS], True, True))
        return (lambda: op("a", [pa], ["aa%d" % k], lambda: A.activation(T.aa[:, e0:e0 + NS], oa, Fn.Identity, bias=float(TT * k))),
                lambda: op("a", [pw], ["ww%d" % k], lambda: A.activation(T.ww[:, e0:e0 + NS], ow, Fn.Identity)))

    def lists(k):
        c, t = slice(24 * k, 24 * k + 24), "%d" % k
        op("v", ["ps"], ["vi" + t], lambda: ts(T.vi[:, c], T.ps[:, 0:24], 65536.0, Op.add))
        op("v", ["ps"], ["em" + t], lambda: ts(T.em[:, c], T.ps[:, 0:24], 0.0, Op.is_equal))
        op("v", ["vi" + t], ["ci" + t], lambda: ts(T.ci[:, c], T.vi[:, c], S - 1, Op.bitwise_and))
        op("v", ["em" + t, "tabd"], ["du" + t], lambda: V.tensor_tensor(T.du[:, c], T.em[:, c], T.tabd[:], Op.mult))
        op("v", ["ci" + t], ["cu" + t], lambda: V.tensor_copy(T.cu[:, c], T.ci[:, c]))
        op("v", ["ci" + t, "du" + t], ["ow" + t], lambda: V.tensor_tensor(T.ow[:, c], T.ci[:, c], T.du[:, c], Op.add))

    def lists2(k):
        c, t = slice(24 * k, 24 * k + 24), "%d" % k
        op("v", ["ow" + t], ["ou" + t], lambda: V.tensor_copy(T.ou[:, c], T.ow[:, c]))
        for j, d in enumerate((-1, 1, -W, W)):
            op("v", ["ci" + t], ["nu%d_%d" % (k, j)], lambda j=j, d=d: ts(
                T.nu[:, 72 * j + 24 * k:72 * j + 24 * k + 24], T.ci[:, c], float(d), Op.add,
                0.0 if d < 0 else float(S - 1), Op.max if d < 0 else Op.min))

    def lgather(k):
        c = slice(NS * k, NS * k + NS)
        op("v", ["lw", "cu%d" % k, "aa%d" % k], ["dt%d" % k], lambda: V.tensor_tensor(
            T.dt[:, c], T.lw[:, 0:S].indirect(T.cu[:, 24 * k:24 * k + 24]), T.aa[:, c], Op.subtract))

    def decay(k):
        c = slice(NS * k, NS * k + NS)
        op("a", ["dt%d" % k, "rat"], ["ee%d" % k], lambda: A.activation(T.ee[:, c], T.dt[:, c], Fn.Exp, scale=T.rat[:]))

    def lscatter(k):
        op("v", ["ou%d" % k, "aa%d" % k], ["lw"], lambda: V.tensor_copy(
            T.lw[:, 0:S + NS].indirect(T.ou[:, 24 * k:24 * k + 24]), T.aa[:, NS * k:NS * k + NS]))

    def vgather(k):
        c = slice(NS * k, NS * k + NS)
        op("v", ["vw", "cu%d" % k, "ee%d" % k], ["tv%d" % k], lambda: V.tensor_tensor(
            T.tv[:, c], T.vw[:, 0:S].indirect(T.cu[:, 24 * k:24 * k + 24]), T.ee[:, c], Op.mult))

    def vscatter(k):
        c = slice(NS * k, NS * k + NS)
        op("v", ["ou%d" % k, "tv%d" % k, "ww%d" % k], ["vw"], lambda: V.tensor_tensor(
            T.vw[:, 0:S + NS].indirect(T.ou[:, 24 * k:24 * k + 24]), T.tv[:, c], T.ww[:, c], Op.add))

    def nlist(k, j, a=0, b=24):
        return T.vw[:, 0:S].indirect(T.nu[:, 72 * j + 24 * k + a:72 * j + 24 * k + b])

    def gbuf(k, j):
        return T.gg[:, NS * (4 * k + j):NS * (4 * k + j + 1)]

    def near(k, j):
        op("a", ["vw", "nu%d_%d" % (k, j)], ["gg%d_%d" % (k, j)], lambda: A.activation(gbuf(k, j), nlist(k, j), Fn.Identity))

    def near_add(k, j, i):
        op("v", ["vw", "nu%d_%d" % (k, j), "gg%d_%d" % (k, i)], ["gg%d_%d" % (k, j)],
           lambda: V.tensor_tensor(gbuf(k, j), nlist(k, j), gbuf(k, i), Op.add))

    def addup(k, order):
        px = "px%d" % k
        for n, j in enumerate(order):
            op("t", ["idn", "gg%d_%d" % (k, j)], [px], lambda n=n, j=j: PE.matmul(
                T[px][:, 0:NS], T.idn[:], gbuf(k, j), n == 0, n == len(order) - 1))

    def slots(k, a=0, b=N):
        return T.ans[:, CAP * a:CAP * b] if k == 0 else T.ans[:, NS + 2 * CAP * a + k - 1:NS + 2 * CAP * b:2]

    def keep(q, m, rd):
        src, dst = sides(T, m)
        op(q, rd, ["rao" + m], (lambda: A.activation(dst(r), src(r, r + 1), Fn.Identity)) if q == "a"
           else (lambda: V.tensor_copy(dst(r), src(r, r + 1))))
        lastw["r" + m] = ("ar_" + m, arrivals(m, r, T, topo))

    def answer(k):
        px = "px%d" % k
        op("a", [px], ["ans%d" % k], lambda: A.activation(slots(k), T[px][:, 0:NS], Fn.Identity))

    def finish(q, k):
        m = "a0" if k == 0 else "a1"
        out = T.yo[:, E * k:E * k + E]
        src = (T.ra[:, 0:NS] if k == 0 else T.ra[:, NS:3 * NS]).indirect(T.sn[:, 16 * k:16 * k + 16])
        op(q, ["r" + m, "rao" + m, "sn%d" % k], ["yo%d" % k],
           (lambda: A.activation(out, src, Fn.Identity)) if q == "a" else (lambda: V.tensor_copy(out, src)))

    places(0)
    ca, cw = times(0); ca(); cw()
    lists(0); lgather(0); decay(0); lists2(0); lscatter(0); vgather(0)
    places(1)
    a1, w1 = times(1)
    a1()
    vscatter(0)
    near(0, 0)
    lists(1); lgather(1); near(0, 1); decay(1); w1(); lists2(1); near_add(0, 3, 0); near(0, 2)
    vgather(1)
    places(2)
    a2, w2 = times(2)
    addup(0, (1, 3, 2))
    a2(); w2()
    vscatter(1)
    near(1, 0); near(1, 1)
    answer(0)
    hand("a0", ["ans0"]); direct("a0", ["ans0"])
    lscatter(1); lists(2); lgather(2); near(1, 2); decay(2); near(1, 3); lists2(2)
    addup(1, (0, 1, 2, 3))
    vgather(2); vscatter(2)
    keep("a", "a0", ["ans0"])
    H = NS // 2
    halves = (1, 0) if r < N // 2 else (0, 1)
    for h in halves:
        op("a", ["vw", "nu2_0"], ["g2_0%d" % h], lambda h=h: A.activation(
            T.gg[:, 8 * NS + H * h:8 * NS + H * h + H], nlist(2, 0, 12 * h, 12 * h + 12), Fn.Identity))
    answer(1)
    for h in halves:
        for j in range(1, 4):
            out = T.gg[:, (8 + j) * NS + H * h:(8 + j) * NS + H * h + H] if j < 3 else slots(2, 4 * h, 4 * h + 4)
            op("v", ["vw", "nu2_%d" % j, "g2_%d%d" % (j - 1, h)], ["g2_%d%d" % (j, h)], lambda h=h, j=j, out=out: V.tensor_tensor(
                out, nlist(2, j, 12 * h, 12 * h + 12), T.gg[:, (7 + j) * NS + H * h:(7 + j) * NS + H * h + H], Op.add))
        if h == halves[0]:
            hand("a1", ["ans1", "g2_3%d" % h])
    direct("a1", ["ans1", "g2_30", "g2_31"])
    keep("v", "a1", ["ans1", "g2_30", "g2_31"])
    finish("a", 0)
    dma("a", "d_y", 2, ["yo0"], [], T.y[:, 0:E], T.yo[:, 0:E])
    finish("a", 1); finish("v", 2)
    dma("s", "d_y", 2, ["yo1", "yo2"], [], T.y[:, E:3 * E], T.yo[:, E:3 * E])

    for s, c in list(cnt.items()) + list(dcnt.items()) + list(sent.items()):
        wait("g", (s, c))
